import numpy as np
import ml_dtypes


def mxq(x, axis, fmt="e4m3"):
    dtype, down = {"e4m3": (ml_dtypes.float8_e4m3fn, 7), "e5m2": (ml_dtypes.float8_e5m2, 14)}[fmt]
    v = np.moveaxis(np.asarray(x, np.float32).astype(ml_dtypes.bfloat16).astype(np.float64), axis, -1)
    blocks = v.reshape(v.shape[:-1] + (-1, 32))
    amax = np.abs(blocks).max(-1, keepdims=True)
    byte = np.maximum(np.where(amax > 0, np.frexp(amax)[1] - 1 + 127, 0) - down, 1)
    scale = np.exp2(byte - 127.0)
    codes = (blocks / scale).astype(np.float32).astype(dtype).astype(np.float64)
    return np.moveaxis((codes * scale).reshape(v.shape), -1, axis)


WIDE = False


def mx_kscale(k):
    if not WIDE:
        return np.ones(k)
    levels = np.array([10, -10, 5, -5, 0])
    if k % 512:
        return np.exp2(np.random.permutation(np.resize(levels, k // 32))).repeat(32)
    a = np.empty((k // 512, 16))
    for p in range(k // 512):
        a[p, :8] = np.random.permutation(np.resize(levels, 8))
        for g in range(8):
            far = levels[np.abs(levels - a[p, g]) >= 10]
            a[p, g + 8] = far[np.random.randint(len(far))]
    return np.exp2(a.ravel()).repeat(32)


def f64(x):
    return np.asarray(x).astype(np.float64)


def striped(idx):
    return np.tile(idx.reshape(-1, 16).T, (8, 1)).astype(np.uint16)


def unstriped(offs):
    return offs[:16].T.reshape(-1).astype(np.int64)


E2M1 = np.array([0.0, 0.5, 1.0, 1.5, 2.0, 3.0, 4.0, 6.0, -0.0, -0.5, -1.0, -1.5, -2.0, -3.0, -4.0, -6.0])


def pack_weight(w, fmt):
    k, n = w.shape
    w = f64(np.asarray(w, np.float32).astype(ml_dtypes.bfloat16)).reshape(k // 32, 32, n)
    amax = np.abs(w).max(1)
    if fmt == "e4m3":
        byte = np.frexp(amax)[1] - 1 + 127 - 7
    else:
        mant, ex = np.frexp(amax / 6.0)
        byte = np.where(mant > 0.5, ex, ex - 1) + 127
    byte = np.clip(np.where(amax > 0, byte, 1), 1, 254)
    scaled = (w * np.exp2(127.0 - byte)[:, None, :]).reshape(k, n).astype(np.float32)
    by_word = np.ascontiguousarray(scaled.reshape(k // 512, 128, 4, n).transpose(0, 1, 3, 2))
    if fmt == "e4m3":
        words = by_word.astype(ml_dtypes.float8_e4m3fn).view(np.uint8)
    else:
        c = by_word.astype(ml_dtypes.float4_e2m1fn).view(np.uint8) & 0xF
        words = (c[..., 0::2] | (c[..., 1::2] << 4)).reshape(k // 512, 128, 2 * n)
    return np.ascontiguousarray(words), np.ascontiguousarray(byte.astype(np.uint8).reshape(k // 512, 16, n))


def unpack_weight(words, scales, fmt):
    g, _, n = scales.shape
    words = np.ascontiguousarray(words).reshape(g, 128, n, -1)
    if fmt == "e4m3":
        vals = words.view(ml_dtypes.float8_e4m3fn).astype(np.float64)
    else:
        nib = np.empty((g, 128, n, 4), np.uint8)
        nib[..., 0::2] = words & 0xF
        nib[..., 1::2] = words >> 4
        vals = E2M1[nib]
    vals = vals * np.repeat(np.exp2(scales.astype(np.float64) - 127.0), 8, axis=1)[..., None]
    return vals.transpose(0, 1, 3, 2).reshape(g * 512, n)


def gelu(v):
    return 0.5 * v * (1.0 + np.tanh(np.sqrt(2.0 / np.pi) * (v + 0.044715 * v**3)))


def often(T, S):
    return np.random.permutation(T)[(T * np.random.uniform(0, 1, S) ** 4).astype(np.int64)]


K, M, H, T, S, P = 1024, 512, 512, 2048, 1024, 512

def setup_inputs():
    n = np.random.standard_normal
    s = mx_kscale(K)[:, None]
    s2 = mx_kscale(M)[:, None]
    u = mx_kscale(H)[:, None]
    d = {}
    d["tab_words"], d["tab_scales"] = pack_weight(n((K, T)) * s, "e4m3")
    d["tab2_words"], d["tab2_scales"] = pack_weight(n((M, T)) * s2, "e4m3")
    d["tab3_words"], d["tab3_scales"] = pack_weight(n((M, T)) * s2, "e4m3")
    d["offs"] = striped(np.random.permutation(T)[:S])
    d["offs2"] = striped(np.random.permutation(T)[:S])
    d["offs3"] = striped(np.random.permutation(T)[:S])
    d["pos1"] = striped(np.random.permutation(S)[:P])
    d["pos2"] = striped(often(S, P))
    d["pos3"] = striped(often(S, P))
    d["wa"] = (n((K, H)) / K**0.5 / s * u.T).astype(np.float32)
    d["wb_words"], d["wb_scales"] = pack_weight(n((M, H)) / M**0.5 / s2 * u.T, "e2m1")
    d["hb"] = (0.7 * n(H) * u[:, 0]).astype(np.float32)
    d["wd"] = (n((M, H)) / M**0.5 / s2 * u.T).astype(np.float32)
    d["wz_words"], d["wz_scales"] = pack_weight(n((H, H)) / H**0.5 / u, "e4m3")
    d["gz"] = (np.exp(0.3 * n(H)) / u[:, 0]).astype(np.float32)
    return d

def reference(tab_words, tab_scales, tab2_words, tab2_scales, tab3_words, tab3_scales, offs, offs2, offs3, pos1, pos2, pos3, wa, wb_words, wb_scales, hb, wd, wz_words, wz_scales, gz):
    v = unpack_weight(tab_words, tab_scales, "e4m3")[:, unstriped(offs)]
    v2 = unpack_weight(tab2_words, tab2_scales, "e4m3")[:, unstriped(offs2)]
    v3 = unpack_weight(tab3_words, tab3_scales, "e4m3")[:, unstriped(offs3)]
    a = mxq(f64(wa), 0, "e4m3").T @ v
    b = (unpack_weight(wb_words, wb_scales, "e2m1").T @ v2) + f64(hb)[:, None]
    d = mxq(f64(wd), 0, "e4m3").T @ v3
    z = a[:, unstriped(pos1)] + np.abs(b[:, unstriped(pos2)]) - np.abs(d[:, unstriped(pos3)])
    y = unpack_weight(wz_words, wz_scales, "e4m3").T @ mxq(z, 0, "e4m3")
    return np.maximum(y, f64(gz)[:, None] * z)

@@ -1,0 +1,221 @@
+from contextlib import ExitStack
+
+import concourse.mybir as mybir
+
+K, M, H, T, S, J = 1024, 512, 512, 2048, 1024, 512
+FLOPS = 2 * H * (K * S + 2 * M * S + H * J)
+
+F32 = mybir.dt.float32
+BF16 = mybir.dt.bfloat16
+I32 = mybir.dt.int32
+U32 = mybir.dt.uint32
+U16 = mybir.dt.uint16
+U8 = mybir.dt.uint8
+FP8X4 = mybir.dt.float8_e4m3fn_x4
+FP4X4 = mybir.dt.float4_e2m1fn_x4
+ALU = mybir.AluOpType
+ACT = mybir.ActivationFunctionType
+
+P = 128
+PACK = 4
+BANK = 512
+BLOCKS = (256, 128, 128)
+
+
+def tile_list_tunnel_drag_join_kernel(
+    tc, tab_words, tab_scales, tab2_words, tab2_scales, tab3_words, tab3_scales,
+    offs, offs2, offs3, pos1, pos2, pos3, wa, wb_words, wb_scales, hb, wd,
+    wz_words, wz_scales, gz, out,
+):
+    nc = tc.nc
+    with ExitStack() as ctx:
+        lists = ctx.enter_context(tc.tile_pool(name="lists", bufs=1))
+        sb = ctx.enter_context(tc.tile_pool(name="sb", bufs=1))
+        shared = ctx.enter_context(tc.tile_pool(name="shared", bufs=1))
+        psum = ctx.enter_context(tc.psum_pool(name="psum", bufs=8))
+
+        def load_list(src, name):
+            tile = lists.tile(list(src.shape), U16, name=name)
+            nc.sync.dma_start(tile[:], src)
+            return tile
+
+        def zeroed_plane(width, name):
+            plane = sb.tile([P, width], U8, name=name, align_bytes=64)
+            nc.vector.memset(plane[:].bitcast(I32), 0)
+            return plane
+
+        def load_scale_rows(plane, src, first):
+            rows = src.shape[0] * 4
+            for q in range(4):
+                nc.sync.dma_start(
+                    plane[32 * q + first : 32 * q + first + rows, :].bitcast(I32),
+                    src[:, 4 * q : 4 * q + 4, :].bitcast(I32),
+                )
+
+        def load_words(src, name):
+            tile = sb.tile([P, src.shape[1]], I32, name=name, align_bytes=64)
+            nc.sync.dma_start(tile[:], src.rearrange("p c i -> p (c i)").bitcast(I32))
+            return tile
+
+        def load_weight(dst, src):
+            nc.sync.dma_start(dst, src.rearrange("(p j) c -> p j c", j=PACK))
+
+        def load_channels(src, name):
+            tile = sb.tile([P, PACK], F32, name=name)
+            nc.sync.dma_start(tile[:], src.rearrange("(p t) -> p t", t=PACK))
+            return tile
+
+        s2_win = zeroed_plane(T, "s2_win")
+        ws_raw = zeroed_plane(H, "ws_raw")
+        s3_win = zeroed_plane(T, "s3_win")
+        s1_win = zeroed_plane(T, "s1_win")
+
+        wb_raw = sb.tile([P, 2 * H], U8, align_bytes=64)
+        nc.sync.dma_start(wb_raw[:].bitcast(I32), wb_words[0].bitcast(I32))
+        wz_raw = load_words(wz_words[0], "wz_raw")
+        offs2_t = load_list(offs2, "offs2_t")
+        load_scale_rows(s2_win, tab2_scales, 0)
+        w2_win = load_words(tab2_words[0], "w2_win")
+        load_scale_rows(ws_raw, wb_scales, 0)
+        load_scale_rows(ws_raw, wz_scales, 4)
+        wd_raw = sb.tile([P, PACK, H], F32, align_bytes=64)
+        load_weight(wd_raw[:], wd)
+        hb_t = load_channels(hb, "hb_t")
+        offs3_t = load_list(offs3, "offs3_t")
+        load_scale_rows(s3_win, tab3_scales, 0)
+        w3_win = load_words(tab3_words[0], "w3_win")
+        offs1_t = load_list(offs, "offs1_t")
+        load_scale_rows(s1_win, tab_scales, 0)
+        wa_raw = shared.tile([P, 2, PACK, H], F32, align_bytes=64, offset=0)
+        for g in range(2):
+            load_weight(wa_raw[:, g], wa[512 * g : 512 * (g + 1), :])
+        pos2_t = load_list(pos2, "pos2_t")
+        w1_win = [load_words(tab_words[g], "w1_win%d" % g) for g in range(2)]
+        pos3_t = load_list(pos3, "pos3_t")
+        pos1_t = load_list(pos1, "pos1_t")
+        gz_t = load_channels(gz, "gz_t")
+
+        wb_codes = sb.tile([P, 2 * H], U8, align_bytes=64)
+        nc.vector.tensor_copy(
+            wb_codes[:].rearrange("p (t m b) -> p t m b", t=PACK, b=2),
+            wb_raw[:].rearrange("p (m t b) -> p t m b", t=PACK, b=2),
+        )
+        wz_codes = sb.tile([P, H], I32, align_bytes=64)
+        nc.vector.tensor_copy(
+            wz_codes[:].rearrange("p (t m) -> p t m", t=PACK),
+            wz_raw[:].rearrange("p (m t) -> p t m", t=PACK),
+        )
+
+        def gather_scales(win, idx, name):
+            tile = sb.tile([P, S], U8, name=name, align_bytes=64)
+            nc.vector.tensor_copy(tile[:], win[:].indirect(idx[:]))
+            return tile
+
+        def gather_words(win, idx, name):
+            tile = sb.tile([P, S], U32, name=name, align_bytes=64)
+            nc.vector.tensor_copy(tile[:], win[:].bitcast(U32).indirect(idx[:]))
+            return tile
+
+        def round_weight(raw, dst):
+            nc.scalar.copy(
+                dst.rearrange("p (t m j) -> p m t j", t=PACK, j=PACK),
+                raw.rearrange("p j (m t) -> p m t j", t=PACK),
+            )
+
+        def quantize(src, width, name):
+            codes = sb.tile([P, width], U32, name=name + "_codes", align_bytes=64)
+            scales = sb.tile([P, width], U8, name=name + "_scales", align_bytes=64)
+            nc.vector.quantize_mx(out=codes[:].bitcast(FP8X4), scales=scales[:], in_=src)
+            return codes, scales
+
+        wd_bf = sb.tile([P, PACK * H], BF16, align_bytes=64)
+        round_weight(wd_raw[:], wd_bf[:])
+        wa_bf = sb.tile([P, 2 * PACK * H], BF16, align_bytes=64)
+        for g in range(2):
+            round_weight(wa_raw[:, g], wa_bf[:, g * PACK * H : (g + 1) * PACK * H])
+
+        v2_scales = gather_scales(s2_win, offs2_t, "v2_scales")
+        v2_codes = gather_words(w2_win, offs2_t, "v2_codes")
+        w_scales = sb.tile([P, H], U8, align_bytes=64)
+        nc.vector.tensor_copy(
+            w_scales[:].rearrange("p (t m) -> p t m", t=PACK),
+            ws_raw[:].rearrange("p (m t) -> p t m", t=PACK),
+        )
+        v3_scales = gather_scales(s3_win, offs3_t, "v3_scales")
+        wd_codes, wd_scales = quantize(wd_bf[:], H, "wd")
+        v3_codes = gather_words(w3_win, offs3_t, "v3_codes")
+        v1_scales = gather_scales(s1_win, offs1_t, "v1_scales")
+        wa_q = [quantize(wa_bf[:, g * PACK * H : (g + 1) * PACK * H], H, "wa%d" % g) for g in range(2)]
+        v1_codes = [gather_words(w1_win[g], offs1_t, "v1_codes%d" % g) for g in range(2)]
+
+        def first_stage(rows, passes, func, bias):
+            for t in range(PACK):
+                row = rows[t]
+                for h in range(S // BANK):
+                    cols = slice(h * BANK, (h + 1) * BANK)
+                    acc = psum.tile([P, BANK], F32, name="acc", tag="bank")
+                    for g, (w_codes, w_plane, v_codes, v_plane) in enumerate(passes):
+                        nc.tensor.matmul_mx(
+                            out=acc[:], lhsT=w_codes(t), lhsT_scale=w_plane(t),
+                            rhs=v_codes[:, cols].bitcast(FP8X4), rhs_scale=v_plane(cols),
+                            start=(g == 0), stop=(g == len(passes) - 1),
+                        )
+                    if bias is None:
+                        nc.scalar.activation(row[:, cols], acc[:], func)
+                    else:
+                        nc.scalar.activation(row[:, cols], acc[:], func, bias=bias[:, t : t + 1])
+
+        def slice_of(tile, dtype=None, size=1):
+            if dtype is None:
+                return lambda t: tile[:, t * P : (t + 1) * P]
+            return lambda t: tile[:, size * t * P : size * (t + 1) * P].bitcast(dtype)
+
+        b_abs = [sb.tile([P, S], F32, name="b_abs%d" % t, align_bytes=64) for t in range(PACK)]
+        first_stage(
+            b_abs, [(slice_of(wb_codes, FP4X4, 2), slice_of(w_scales), v2_codes, lambda c: v2_scales[:, c])],
+            ACT.Abs, hb_t)
+        d_abs = [shared.tile([P, S], F32, name="d_abs%d" % t, align_bytes=64, offset=4 * S * t) for t in range(PACK)]
+        first_stage(
+            d_abs, [(slice_of(wd_codes, FP8X4), slice_of(wd_scales), v3_codes, lambda c: v3_scales[:, c])],
+            ACT.Abs, None)
+        a_rows = [sb.tile([P, S], F32, name="a_rows%d" % t, align_bytes=64) for t in range(PACK)]
+        first_stage(
+            a_rows,
+            [(slice_of(wa_q[0][0], FP8X4), slice_of(wa_q[0][1]), v1_codes[0], lambda c: v1_scales[:, c]),
+             (slice_of(wa_q[1][0], FP8X4), slice_of(wa_q[1][1]), v1_codes[1], lambda c: v1_scales[4:P, c])],
+            ACT.Copy, None)
+
+        b_pick = sb.tile([P, PACK, J], F32, align_bytes=64)
+        for t in range(PACK):
+            nc.vector.tensor_copy(b_pick[:, t, :], b_abs[t][:].indirect(pos2_t[:]))
+        db = sb.tile([P, PACK, J], F32, align_bytes=64)
+        for t in range(PACK):
+            nc.vector.tensor_tensor(db[:, t, :], d_abs[t][:].indirect(pos3_t[:]), b_pick[:, t, :], ALU.subtract)
+
+        out_rows = out.rearrange("(p t) j -> p t j", t=PACK)
+        j0 = 0
+        for n, width in enumerate(BLOCKS):
+            cols = slice(j0, j0 + width)
+            z = sb.tile([P, PACK, width], F32, name="z%d" % n, align_bytes=64)
+            for t in range(PACK):
+                nc.vector.tensor_tensor(
+                    z[:, t, :], a_rows[t][:].indirect(pos1_t[:, j0 // 16 : (j0 + width) // 16]), db[:, t, cols], ALU.subtract)
+            z_bf = sb.tile([P, width, PACK], BF16, name="z_bf%d" % n, align_bytes=64)
+            nc.scalar.copy(z_bf[:], z[:].rearrange("p t j -> p j t"))
+            z_codes, z_scales = quantize(z_bf[:].rearrange("p j t -> p (j t)"), width, "z%d" % n)
+            res = sb.tile([P, PACK, width], F32, name="res%d" % n, align_bytes=64)
+            per_bank = BANK // width
+            for t in range(PACK):
+                if t % per_bank == 0:
+                    y = psum.tile([P, per_bank, width], F32, name="y", tag="bank")
+                nc.tensor.matmul_mx(
+                    out=y[:, t % per_bank, :], lhsT=wz_codes[:, t * P : (t + 1) * P].bitcast(FP8X4),
+                    lhsT_scale=w_scales[4:P, t * P : (t + 1) * P],
+                    rhs=z_codes[:].bitcast(FP8X4), rhs_scale=z_scales[:], start=True, stop=True,
+                )
+                if t % per_bank == per_bank - 1:
+                    for u in range(t - per_bank + 1, t + 1):
+                        nc.vector.scalar_tensor_tensor(
+                            res[:, u, :], z[:, u, :], gz_t[:, u : u + 1], y[:, u % per_bank, :], ALU.mult, ALU.max)
+            nc.sync.dma_start(out_rows[:, :, cols], res[:])
+            j0 = j0 + width

@@ -44,16 +44,16 @@ def tile_list_tunnel_drag_join_kernel(
             nc.vector.memset(plane[:].bitcast(I32), 0)
             return plane
 
-        def load_scale_rows(plane, src, first):
+        def load_scale_rows(queue, plane, src, first):
             rows = src.shape[0] * 4
             for q in range(4):
-                nc.sync.dma_start(
+                queue.dma_start(
                     plane[32 * q + first : 32 * q + first + rows, :].bitcast(I32),
                     src[:, 4 * q : 4 * q + 4, :].bitcast(I32),
                 )
 
-        def load_words(src, name):
-            tile = sb.tile([P, src.shape[1]], I32, name=name, align_bytes=64)
+        def load_words(src, name, tag=""):
+            tile = sb.tile([P, src.shape[1]], I32, name=name, tag=tag or name, align_bytes=64)
             nc.sync.dma_start(tile[:], src.rearrange("p c i -> p (c i)").bitcast(I32))
             return tile
 
@@ -74,23 +74,23 @@ def tile_list_tunnel_drag_join_kernel(
         nc.sync.dma_start(wb_raw[:].bitcast(I32), wb_words[0].bitcast(I32))
         wz_raw = load_words(wz_words[0], "wz_raw")
         offs2_t = load_list(offs2, "offs2_t")
-        load_scale_rows(s2_win, tab2_scales, 0)
+        load_scale_rows(nc.sync, s2_win, tab2_scales, 0)
         w2_win = load_words(tab2_words[0], "w2_win")
-        load_scale_rows(ws_raw, wb_scales, 0)
-        load_scale_rows(ws_raw, wz_scales, 4)
+        load_scale_rows(nc.sync, ws_raw, wb_scales, 0)
         wd_raw = sb.tile([P, PACK, H], F32, align_bytes=64)
         load_weight(wd_raw[:], wd)
+        load_scale_rows(nc.sync, ws_raw, wz_scales, 4)
         hb_t = load_channels(hb, "hb_t")
-        offs3_t = load_list(offs3, "offs3_t")
-        load_scale_rows(s3_win, tab3_scales, 0)
-        w3_win = load_words(tab3_words[0], "w3_win")
-        offs1_t = load_list(offs, "offs1_t")
-        load_scale_rows(s1_win, tab_scales, 0)
         wa_raw = shared.tile([P, 2, PACK, H], F32, align_bytes=64, offset=0)
-        for g in range(2):
-            load_weight(wa_raw[:, g], wa[512 * g : 512 * (g + 1), :])
+        load_weight(wa_raw[:, 0], wa[0:512, :])
+        offs3_t = load_list(offs3, "offs3_t")
+        load_scale_rows(nc.sync, s3_win, tab3_scales, 0)
+        load_weight(wa_raw[:, 1], wa[512:1024, :])
+        offs1_t = load_list(offs, "offs1_t")
+        load_scale_rows(nc.sync, s1_win, tab_scales, 0)
         pos2_t = load_list(pos2, "pos2_t")
-        w1_win = [load_words(tab_words[g], "w1_win%d" % g) for g in range(2)]
+        w3_win = load_words(tab3_words[0], "w3_win")
+        w1_win = [load_words(tab_words[0], "w1_win0"), load_words(tab_words[1], "w1_win1", "last_window")]
         pos3_t = load_list(pos3, "pos3_t")
         pos1_t = load_list(pos1, "pos1_t")
         gz_t = load_channels(gz, "gz_t")
@@ -102,8 +102,8 @@ def tile_list_tunnel_drag_join_kernel(
         )
         wz_codes = sb.tile([P, H], I32, align_bytes=64)
         nc.vector.tensor_copy(
-            wz_codes[:].rearrange("p (t m) -> p t m", t=PACK),
-            wz_raw[:].rearrange("p (m t) -> p t m", t=PACK),
+            wz_codes[:].rearrange("p (t m) -> p m t", t=PACK),
+            wz_raw[:].rearrange("p (m t) -> p m t", t=PACK),
         )
 
         def gather_scales(win, idx, name):
@@ -122,8 +122,8 @@ def tile_list_tunnel_drag_join_kernel(
                 raw.rearrange("p j (m t) -> p m t j", t=PACK),
             )
 
-        def quantize(src, width, name):
-            codes = sb.tile([P, width], U32, name=name + "_codes", align_bytes=64)
+        def quantize(src, width, name, tag=""):
+            codes = sb.tile([P, width], U32, name=name + "_codes", tag=tag or name + "_codes", align_bytes=64)
             scales = sb.tile([P, width], U8, name=name + "_scales", align_bytes=64)
             nc.vector.quantize_mx(out=codes[:].bitcast(FP8X4), scales=scales[:], in_=src)
             return codes, scales
@@ -145,8 +145,14 @@ def tile_list_tunnel_drag_join_kernel(
         wd_codes, wd_scales = quantize(wd_bf[:], H, "wd")
         v3_codes = gather_words(w3_win, offs3_t, "v3_codes")
         v1_scales = gather_scales(s1_win, offs1_t, "v1_scales")
-        wa_q = [quantize(wa_bf[:, g * PACK * H : (g + 1) * PACK * H], H, "wa%d" % g) for g in range(2)]
         v1_codes = [gather_words(w1_win[g], offs1_t, "v1_codes%d" % g) for g in range(2)]
+        wa_codes = sb.tile([P, 2, H], U32, tag="w1_win0", align_bytes=64)
+        wa_scales = sb.tile([P, 2, H], U8, align_bytes=64)
+        for g in range(2):
+            nc.vector.quantize_mx(
+                out=wa_codes[:, g, :].bitcast(FP8X4), scales=wa_scales[:, g, :],
+                in_=wa_bf[:, g * PACK * H : (g + 1) * PACK * H])
+        wa_q = [(wa_codes[:, g, :], wa_scales[:, g, :]) for g in range(2)]
 
         def first_stage(rows, passes, func, bias):
             for t in range(PACK):
@@ -185,10 +191,10 @@ def tile_list_tunnel_drag_join_kernel(
              (slice_of(wa_q[1][0], FP8X4), slice_of(wa_q[1][1]), v1_codes[1], lambda c: v1_scales[4:P, c])],
             ACT.Copy, None)
 
-        b_pick = sb.tile([P, PACK, J], F32, align_bytes=64)
+        b_pick = sb.tile([P, PACK, J], F32, tag="w3_win", align_bytes=64)
         for t in range(PACK):
             nc.vector.tensor_copy(b_pick[:, t, :], b_abs[t][:].indirect(pos2_t[:]))
-        db = sb.tile([P, PACK, J], F32, align_bytes=64)
+        db = sb.tile([P, PACK, J], F32, tag="last_window", align_bytes=64)
         for t in range(PACK):
             nc.vector.tensor_tensor(db[:, t, :], d_abs[t][:].indirect(pos3_t[:]), b_pick[:, t, :], ALU.subtract)
 

@@ -66,44 +66,48 @@ def tile_list_tunnel_drag_join_kernel(
             return tile
 
         s2_win = zeroed_plane(T, "s2_win")
-        ws_raw = zeroed_plane(H, "ws_raw")
+        wbs_raw = zeroed_plane(H, "wbs_raw")
         s3_win = zeroed_plane(T, "s3_win")
         s1_win = zeroed_plane(T, "s1_win")
+        wzs_raw = zeroed_plane(H, "wzs_raw")
 
         wb_raw = sb.tile([P, 2 * H], U8, align_bytes=64)
         nc.sync.dma_start(wb_raw[:].bitcast(I32), wb_words[0].bitcast(I32))
-        wz_raw = load_words(wz_words[0], "wz_raw")
+        pos2_t = load_list(pos2, "pos2_t")
         offs2_t = load_list(offs2, "offs2_t")
         load_scale_rows(nc.sync, s2_win, tab2_scales, 0)
         w2_win = load_words(tab2_words[0], "w2_win")
-        load_scale_rows(nc.sync, ws_raw, wb_scales, 0)
+        load_scale_rows(nc.sync, wbs_raw, wb_scales, 0)
         wd_raw = sb.tile([P, PACK, H], F32, align_bytes=64)
         load_weight(wd_raw[:], wd)
-        load_scale_rows(nc.sync, ws_raw, wz_scales, 4)
         hb_t = load_channels(hb, "hb_t")
-        wa_raw = shared.tile([P, 2, PACK, H], F32, align_bytes=64, offset=0)
-        load_weight(wa_raw[:, 0], wa[0:512, :])
         offs3_t = load_list(offs3, "offs3_t")
         load_scale_rows(nc.sync, s3_win, tab3_scales, 0)
-        load_weight(wa_raw[:, 1], wa[512:1024, :])
+        w3_win = load_words(tab3_words[0], "w3_win")
         offs1_t = load_list(offs, "offs1_t")
         load_scale_rows(nc.sync, s1_win, tab_scales, 0)
-        pos2_t = load_list(pos2, "pos2_t")
-        w3_win = load_words(tab3_words[0], "w3_win")
-        w1_win = [load_words(tab_words[0], "w1_win0"), load_words(tab_words[1], "w1_win1", "last_window")]
+        wa_raw = shared.tile([P, 2, PACK, H], F32, align_bytes=64, offset=0)
+        load_weight(wa_raw[:, 0], wa[0:512, :])
+        load_weight(wa_raw[:, 1], wa[512:1024, :])
+        wz_raw = load_words(wz_words[0], "wz_raw")
+        load_scale_rows(nc.sync, wzs_raw, wz_scales, 0)
+        w1_win = [load_words(tab_words[0], "w1_win0"), load_words(tab_words[1], "w1_win1")]
         pos3_t = load_list(pos3, "pos3_t")
         pos1_t = load_list(pos1, "pos1_t")
         gz_t = load_channels(gz, "gz_t")
 
+        def deal_scales(engine, raw, name):
+            plane = sb.tile([P, H], U8, name=name, align_bytes=64)
+            engine.tensor_copy(
+                plane[:].rearrange("p (t m) -> p t m", t=PACK),
+                raw[:].rearrange("p (m t) -> p t m", t=PACK),
+            )
+            return plane
+
         wb_codes = sb.tile([P, 2 * H], U8, align_bytes=64)
         nc.vector.tensor_copy(
-            wb_codes[:].rearrange("p (t m b) -> p t m b", t=PACK, b=2),
-            wb_raw[:].rearrange("p (m t b) -> p t m b", t=PACK, b=2),
-        )
-        wz_codes = sb.tile([P, H], I32, align_bytes=64)
-        nc.vector.tensor_copy(
-            wz_codes[:].rearrange("p (t m) -> p m t", t=PACK),
-            wz_raw[:].rearrange("p (m t) -> p m t", t=PACK),
+            wb_codes[:].bitcast(U16).rearrange("p (t m) -> p t m", t=PACK),
+            wb_raw[:].bitcast(U16).rearrange("p (m t) -> p t m", t=PACK),
         )
 
         def gather_scales(win, idx, name):
@@ -136,17 +140,13 @@ def tile_list_tunnel_drag_join_kernel(
 
         v2_scales = gather_scales(s2_win, offs2_t, "v2_scales")
         v2_codes = gather_words(w2_win, offs2_t, "v2_codes")
-        w_scales = sb.tile([P, H], U8, align_bytes=64)
-        nc.vector.tensor_copy(
-            w_scales[:].rearrange("p (t m) -> p t m", t=PACK),
-            ws_raw[:].rearrange("p (m t) -> p t m", t=PACK),
-        )
+        wb_plane = deal_scales(nc.gpsimd, wbs_raw, "wb_plane")
         v3_scales = gather_scales(s3_win, offs3_t, "v3_scales")
         wd_codes, wd_scales = quantize(wd_bf[:], H, "wd")
         v3_codes = gather_words(w3_win, offs3_t, "v3_codes")
         v1_scales = gather_scales(s1_win, offs1_t, "v1_scales")
         v1_codes = [gather_words(w1_win[g], offs1_t, "v1_codes%d" % g) for g in range(2)]
-        wa_codes = sb.tile([P, 2, H], U32, tag="w1_win0", align_bytes=64)
+        wa_codes = sb.tile([P, 2, H], U32, align_bytes=64)
         wa_scales = sb.tile([P, 2, H], U8, align_bytes=64)
         for g in range(2):
             nc.vector.quantize_mx(
@@ -178,7 +178,7 @@ def tile_list_tunnel_drag_join_kernel(
 
         b_abs = [sb.tile([P, S], F32, name="b_abs%d" % t, align_bytes=64) for t in range(PACK)]
         first_stage(
-            b_abs, [(slice_of(wb_codes, FP4X4, 2), slice_of(w_scales), v2_codes, lambda c: v2_scales[:, c])],
+            b_abs, [(slice_of(wb_codes, FP4X4, 2), slice_of(wb_plane), v2_codes, lambda c: v2_scales[:, c])],
             ACT.Abs, hb_t)
         d_abs = [shared.tile([P, S], F32, name="d_abs%d" % t, align_bytes=64, offset=4 * S * t) for t in range(PACK)]
         first_stage(
@@ -191,12 +191,19 @@ def tile_list_tunnel_drag_join_kernel(
              (slice_of(wa_q[1][0], FP8X4), slice_of(wa_q[1][1]), v1_codes[1], lambda c: v1_scales[4:P, c])],
             ACT.Copy, None)
 
-        b_pick = sb.tile([P, PACK, J], F32, tag="w3_win", align_bytes=64)
+        b_pick = sb.tile([P, PACK, J], F32, align_bytes=64)
         for t in range(PACK):
             nc.vector.tensor_copy(b_pick[:, t, :], b_abs[t][:].indirect(pos2_t[:]))
-        db = sb.tile([P, PACK, J], F32, tag="last_window", align_bytes=64)
+        db = sb.tile([P, PACK, J], F32, tag="w1_win1", align_bytes=64)
         for t in range(PACK):
             nc.vector.tensor_tensor(db[:, t, :], d_abs[t][:].indirect(pos3_t[:]), b_pick[:, t, :], ALU.subtract)
+
+        wz_codes = sb.tile([P, H], I32, align_bytes=64)
+        nc.gpsimd.tensor_copy(
+            wz_codes[:].rearrange("p (t m) -> p m t", t=PACK),
+            wz_raw[:].rearrange("p (m t) -> p m t", t=PACK),
+        )
+        wz_plane = deal_scales(nc.gpsimd, wzs_raw, "wz_plane")
 
         out_rows = out.rearrange("(p t) j -> p t j", t=PACK)
         j0 = 0
@@ -208,20 +215,21 @@ def tile_list_tunnel_drag_join_kernel(
                     z[:, t, :], a_rows[t][:].indirect(pos1_t[:, j0 // 16 : (j0 + width) // 16]), db[:, t, cols], ALU.subtract)
             z_bf = sb.tile([P, width, PACK], BF16, name="z_bf%d" % n, align_bytes=64)
             nc.scalar.copy(z_bf[:], z[:].rearrange("p t j -> p j t"))
+            gated = sb.tile([P, PACK, width], F32, name="gated%d" % n, align_bytes=64)
+            for t in range(PACK):
+                nc.scalar.activation(gated[:, t, :], z[:, t, :], ACT.Copy, scale=gz_t[:, t : t + 1])
             z_codes, z_scales = quantize(z_bf[:].rearrange("p j t -> p (j t)"), width, "z%d" % n)
             res = sb.tile([P, PACK, width], F32, name="res%d" % n, align_bytes=64)
-            per_bank = BANK // width
-            for t in range(PACK):
-                if t % per_bank == 0:
-                    y = psum.tile([P, per_bank, width], F32, name="y", tag="bank")
-                nc.tensor.matmul_mx(
-                    out=y[:, t % per_bank, :], lhsT=wz_codes[:, t * P : (t + 1) * P].bitcast(FP8X4),
-                    lhsT_scale=w_scales[4:P, t * P : (t + 1) * P],
-                    rhs=z_codes[:].bitcast(FP8X4), rhs_scale=z_scales[:], start=True, stop=True,
-                )
-                if t % per_bank == per_bank - 1:
-                    for u in range(t - per_bank + 1, t + 1):
-                        nc.vector.scalar_tensor_tensor(
-                            res[:, u, :], z[:, u, :], gz_t[:, u : u + 1], y[:, u % per_bank, :], ALU.mult, ALU.max)
-            nc.sync.dma_start(out_rows[:, :, cols], res[:])
+            for pair in range(PACK // 2):
+                rows = slice(2 * pair, 2 * pair + 2)
+                y = psum.tile([P, 2, width], F32, name="y", tag="bank")
+                for u in range(2):
+                    t = 2 * pair + u
+                    nc.tensor.matmul_mx(
+                        out=y[:, u, :], lhsT=wz_codes[:, t * P : (t + 1) * P].bitcast(FP8X4),
+                        lhsT_scale=wz_plane[:, t * P : (t + 1) * P],
+                        rhs=z_codes[:].bitcast(FP8X4), rhs_scale=z_scales[:], start=True, stop=True,
+                    )
+                nc.vector.tensor_tensor(res[:, rows, :], y[:], gated[:, rows, :], ALU.max)
+                nc.sync.dma_start(out_rows[:, rows, cols], res[:, rows, :])
             j0 = j0 + width

from contextlib import ExitStack

import concourse.mybir as mybir

K, M, H, T, S, J = 1024, 512, 512, 2048, 1024, 512
FLOPS = 2 * H * (K * S + 2 * M * S + H * J)

F32 = mybir.dt.float32
BF16 = mybir.dt.bfloat16
I32 = mybir.dt.int32
U32 = mybir.dt.uint32
U16 = mybir.dt.uint16
U8 = mybir.dt.uint8
FP8X4 = mybir.dt.float8_e4m3fn_x4
FP4X4 = mybir.dt.float4_e2m1fn_x4
ALU = mybir.AluOpType
ACT = mybir.ActivationFunctionType

P = 128
PACK = 4
BANK = 512
BLOCKS = (256, 128, 128)


def tile_list_tunnel_drag_join_kernel(
    tc, tab_words, tab_scales, tab2_words, tab2_scales, tab3_words, tab3_scales,
    offs, offs2, offs3, pos1, pos2, pos3, wa, wb_words, wb_scales, hb, wd,
    wz_words, wz_scales, gz, out,
):
    nc = tc.nc
    with ExitStack() as ctx:
        lists = ctx.enter_context(tc.tile_pool(name="lists", bufs=1))
        sb = ctx.enter_context(tc.tile_pool(name="sb", bufs=1))
        shared = ctx.enter_context(tc.tile_pool(name="shared", bufs=1))
        psum = ctx.enter_context(tc.psum_pool(name="psum", bufs=8))

        def load_list(src, name):
            tile = lists.tile(list(src.shape), U16, name=name)
            nc.sync.dma_start(tile[:], src)
            return tile

        def zeroed_plane(width, name):
            plane = sb.tile([P, width], U8, name=name, align_bytes=64)
            nc.vector.memset(plane[:].bitcast(I32), 0)
            return plane

        def load_scale_rows(queue, plane, src, first):
            rows = src.shape[0] * 4
            for q in range(4):
                queue.dma_start(
                    plane[32 * q + first : 32 * q + first + rows, :].bitcast(I32),
                    src[:, 4 * q : 4 * q + 4, :].bitcast(I32),
                )

        def load_words(src, name, tag=""):
            tile = sb.tile([P, src.shape[1]], I32, name=name, tag=tag or name, align_bytes=64)
            nc.sync.dma_start(tile[:], src.rearrange("p c i -> p (c i)").bitcast(I32))
            return tile

        def load_weight(dst, src):
            nc.sync.dma_start(dst, src.rearrange("(p j) c -> p j c", j=PACK))

        def load_channels(src, name):
            tile = sb.tile([P, PACK], F32, name=name)
            nc.sync.dma_start(tile[:], src.rearrange("(p t) -> p t", t=PACK))
            return tile

        s2_win = zeroed_plane(T, "s2_win")
        wbs_raw = zeroed_plane(H, "wbs_raw")
        s3_win = zeroed_plane(T, "s3_win")
        s1_win = zeroed_plane(T, "s1_win")
        wzs_raw = zeroed_plane(H, "wzs_raw")

        wb_raw = sb.tile([P, 2 * H], U8, align_bytes=64)
        nc.sync.dma_start(wb_raw[:].bitcast(I32), wb_words[0].bitcast(I32))
        pos2_t = load_list(pos2, "pos2_t")
        offs2_t = load_list(offs2, "offs2_t")
        load_scale_rows(nc.sync, s2_win, tab2_scales, 0)
        w2_win = load_words(tab2_words[0], "w2_win")
        load_scale_rows(nc.sync, wbs_raw, wb_scales, 0)
        wd_raw = sb.tile([P, PACK, H], F32, align_bytes=64)
        load_weight(wd_raw[:], wd)
        hb_t = load_channels(hb, "hb_t")
        offs3_t = load_list(offs3, "offs3_t")
        load_scale_rows(nc.sync, s3_win, tab3_scales, 0)
        w3_win = load_words(tab3_words[0], "w3_win")
        offs1_t = load_list(offs, "offs1_t")
        load_scale_rows(nc.sync, s1_win, tab_scales, 0)
        wa_raw = shared.tile([P, 2, PACK, H], F32, align_bytes=64, offset=0)
        load_weight(wa_raw[:, 0], wa[0:512, :])
        load_weight(wa_raw[:, 1], wa[512:1024, :])
        wz_raw = load_words(wz_words[0], "wz_raw")
        load_scale_rows(nc.sync, wzs_raw, wz_scales, 0)
        w1_win = [load_words(tab_words[0], "w1_win0"), load_words(tab_words[1], "w1_win1")]
        pos3_t = load_list(pos3, "pos3_t")
        pos1_t = load_list(pos1, "pos1_t")
        gz_t = load_channels(gz, "gz_t")

        def deal_scales(engine, raw, name):
            plane = sb.tile([P, H], U8, name=name, align_bytes=64)
            engine.tensor_copy(
                plane[:].rearrange("p (t m) -> p t m", t=PACK),
                raw[:].rearrange("p (m t) -> p t m", t=PACK),
            )
            return plane

        wb_codes = sb.tile([P, 2 * H], U8, align_bytes=64)
        nc.vector.tensor_copy(
            wb_codes[:].bitcast(U16).rearrange("p (t m) -> p t m", t=PACK),
            wb_raw[:].bitcast(U16).rearrange("p (m t) -> p t m", t=PACK),
        )

        def gather_scales(win, idx, name):
            tile = sb.tile([P, S], U8, name=name, align_bytes=64)
            nc.vector.tensor_copy(tile[:], win[:].indirect(idx[:]))
            return tile

        def gather_words(win, idx, name):
            tile = sb.tile([P, S], U32, name=name, align_bytes=64)
            nc.vector.tensor_copy(tile[:], win[:].bitcast(U32).indirect(idx[:]))
            return tile

        def round_weight(raw, dst):
            nc.scalar.copy(
                dst.rearrange("p (t m j) -> p m t j", t=PACK, j=PACK),
                raw.rearrange("p j (m t) -> p m t j", t=PACK),
            )

        def quantize(src, width, name, tag=""):
            codes = sb.tile([P, width], U32, name=name + "_codes", tag=tag or name + "_codes", align_bytes=64)
            scales = sb.tile([P, width], U8, name=name + "_scales", align_bytes=64)
            nc.vector.quantize_mx(out=codes[:].bitcast(FP8X4), scales=scales[:], in_=src)
            return codes, scales

        wd_bf = sb.tile([P, PACK * H], BF16, align_bytes=64)
        round_weight(wd_raw[:], wd_bf[:])
        wa_bf = sb.tile([P, 2 * PACK * H], BF16, align_bytes=64)
        for g in range(2):
            round_weight(wa_raw[:, g], wa_bf[:, g * PACK * H : (g + 1) * PACK * H])

        v2_scales = gather_scales(s2_win, offs2_t, "v2_scales")
        v2_codes = gather_words(w2_win, offs2_t, "v2_codes")
        wb_plane = deal_scales(nc.gpsimd, wbs_raw, "wb_plane")
        v3_scales = gather_scales(s3_win, offs3_t, "v3_scales")
        wd_codes, wd_scales = quantize(wd_bf[:], H, "wd")
        v3_codes = gather_words(w3_win, offs3_t, "v3_codes")
        v1_scales = gather_scales(s1_win, offs1_t, "v1_scales")
        v1_codes = [gather_words(w1_win[g], offs1_t, "v1_codes%d" % g) for g in range(2)]
        wa_codes = sb.tile([P, 2, H], U32, align_bytes=64)
        wa_scales = sb.tile([P, 2, H], U8, align_bytes=64)
        for g in range(2):
            nc.vector.quantize_mx(
                out=wa_codes[:, g, :].bitcast(FP8X4), scales=wa_scales[:, g, :],
                in_=wa_bf[:, g * PACK * H : (g + 1) * PACK * H])
        wa_q = [(wa_codes[:, g, :], wa_scales[:, g, :]) for g in range(2)]

        def first_stage(rows, passes, func, bias):
            for t in range(PACK):
                row = rows[t]
                for h in range(S // BANK):
                    cols = slice(h * BANK, (h + 1) * BANK)
                    acc = psum.tile([P, BANK], F32, name="acc", tag="bank")
                    for g, (w_codes, w_plane, v_codes, v_plane) in enumerate(passes):
                        nc.tensor.matmul_mx(
                            out=acc[:], lhsT=w_codes(t), lhsT_scale=w_plane(t),
                            rhs=v_codes[:, cols].bitcast(FP8X4), rhs_scale=v_plane(cols),
                            start=(g == 0), stop=(g == len(passes) - 1),
                        )
                    if bias is None:
                        nc.scalar.activation(row[:, cols], acc[:], func)
                    else:
                        nc.scalar.activation(row[:, cols], acc[:], func, bias=bias[:, t : t + 1])

        def slice_of(tile, dtype=None, size=1):
            if dtype is None:
                return lambda t: tile[:, t * P : (t + 1) * P]
            return lambda t: tile[:, size * t * P : size * (t + 1) * P].bitcast(dtype)

        b_abs = [sb.tile([P, S], F32, name="b_abs%d" % t, align_bytes=64) for t in range(PACK)]
        first_stage(
            b_abs, [(slice_of(wb_codes, FP4X4, 2), slice_of(wb_plane), v2_codes, lambda c: v2_scales[:, c])],
            ACT.Abs, hb_t)
        d_abs = [shared.tile([P, S], F32, name="d_abs%d" % t, align_bytes=64, offset=4 * S * t) for t in range(PACK)]
        first_stage(
            d_abs, [(slice_of(wd_codes, FP8X4), slice_of(wd_scales), v3_codes, lambda c: v3_scales[:, c])],
            ACT.Abs, None)
        a_rows = [sb.tile([P, S], F32, name="a_rows%d" % t, align_bytes=64) for t in range(PACK)]
        first_stage(
            a_rows,
            [(slice_of(wa_q[0][0], FP8X4), slice_of(wa_q[0][1]), v1_codes[0], lambda c: v1_scales[:, c]),
             (slice_of(wa_q[1][0], FP8X4), slice_of(wa_q[1][1]), v1_codes[1], lambda c: v1_scales[4:P, c])],
            ACT.Copy, None)

        b_pick = sb.tile([P, PACK, J], F32, align_bytes=64)
        for t in range(PACK):
            nc.vector.tensor_copy(b_pick[:, t, :], b_abs[t][:].indirect(pos2_t[:]))
        db = sb.tile([P, PACK, J], F32, tag="w1_win1", align_bytes=64)
        for t in range(PACK):
            nc.vector.tensor_tensor(db[:, t, :], d_abs[t][:].indirect(pos3_t[:]), b_pick[:, t, :], ALU.subtract)

        wz_codes = sb.tile([P, H], I32, align_bytes=64)
        nc.gpsimd.tensor_copy(
            wz_codes[:].rearrange("p (t m) -> p m t", t=PACK),
            wz_raw[:].rearrange("p (m t) -> p m t", t=PACK),
        )
        wz_plane = deal_scales(nc.gpsimd, wzs_raw, "wz_plane")

        out_rows = out.rearrange("(p t) j -> p t j", t=PACK)
        j0 = 0
        for n, width in enumerate(BLOCKS):
            cols = slice(j0, j0 + width)
            z = sb.tile([P, PACK, width], F32, name="z%d" % n, align_bytes=64)
            for t in range(PACK):
                nc.vector.tensor_tensor(
                    z[:, t, :], a_rows[t][:].indirect(pos1_t[:, j0 // 16 : (j0 + width) // 16]), db[:, t, cols], ALU.subtract)
            z_bf = sb.tile([P, width, PACK], BF16, name="z_bf%d" % n, align_bytes=64)
            nc.scalar.copy(z_bf[:], z[:].rearrange("p t j -> p j t"))
            gated = sb.tile([P, PACK, width], F32, name="gated%d" % n, align_bytes=64)
            for t in range(PACK):
                nc.scalar.activation(gated[:, t, :], z[:, t, :], ACT.Copy, scale=gz_t[:, t : t + 1])
            z_codes, z_scales = quantize(z_bf[:].rearrange("p j t -> p (j t)"), width, "z%d" % n)
            res = sb.tile([P, PACK, width], F32, name="res%d" % n, align_bytes=64)
            for pair in range(PACK // 2):
                rows = slice(2 * pair, 2 * pair + 2)
                y = psum.tile([P, 2, width], F32, name="y", tag="bank")
                for u in range(2):
                    t = 2 * pair + u
                    nc.tensor.matmul_mx(
                        out=y[:, u, :], lhsT=wz_codes[:, t * P : (t + 1) * P].bitcast(FP8X4),
                        lhsT_scale=wz_plane[:, t * P : (t + 1) * P],
                        rhs=z_codes[:].bitcast(FP8X4), rhs_scale=z_scales[:], start=True, stop=True,
                    )
                nc.vector.tensor_tensor(res[:, rows, :], y[:], gated[:, rows, :], ALU.max)
                nc.sync.dma_start(out_rows[:, rows, cols], res[:, rows, :])
            j0 = j0 + width
